import numpy as np
import ml_dtypes


def mxq(x, axis, fmt="e4m3"):
    dtype, down = {"e4m3": (ml_dtypes.float8_e4m3fn, 7), "e5m2": (ml_dtypes.float8_e5m2, 14)}[fmt]
    v = np.moveaxis(np.asarray(x, np.float32).astype(ml_dtypes.bfloat16).astype(np.float64), axis, -1)
    blocks = v.reshape(v.shape[:-1] + (-1, 32))
    amax = np.abs(blocks).max(-1, keepdims=True)
    byte = np.maximum(np.where(amax > 0, np.frexp(amax)[1] - 1 + 127, 0) - down, 1)
    scale = np.exp2(byte - 127.0)
    codes = (blocks / scale).astype(np.float32).astype(dtype).astype(np.float64)
    return np.moveaxis((codes * scale).reshape(v.shape), -1, axis)


WIDE = False


def mx_kscale(k):
    if not WIDE:
        return np.ones(k)
    levels = np.array([10, -10, 5, -5, 0])
    if k % 512:
        return np.exp2(np.random.permutation(np.resize(levels, k // 32))).repeat(32)
    a = np.empty((k // 512, 16))
    for p in range(k // 512):
        a[p, :8] = np.random.permutation(np.resize(levels, 8))
        for g in range(8):
            far = levels[np.abs(levels - a[p, g]) >= 10]
            a[p, g + 8] = far[np.random.randint(len(far))]
    return np.exp2(a.ravel()).repeat(32)


def f64(x):
    return np.asarray(x).astype(np.float64)


def striped(idx):
    return np.tile(idx.reshape(-1, 16).T, (8, 1)).astype(np.uint16)


def unstriped(offs):
    return offs[:16].T.reshape(-1).astype(np.int64)


E2M1 = np.array([0.0, 0.5, 1.0, 1.5, 2.0, 3.0, 4.0, 6.0, -0.0, -0.5, -1.0, -1.5, -2.0, -3.0, -4.0, -6.0])


def pack_weight(w, fmt):
    k, n = w.shape
    w = f64(np.asarray(w, np.float32).astype(ml_dtypes.bfloat16)).reshape(k // 32, 32, n)
    amax = np.abs(w).max(1)
    if fmt == "e4m3":
        byte = np.frexp(amax)[1] - 1 + 127 - 7
    else:
        mant, ex = np.frexp(amax / 6.0)
        byte = np.where(mant > 0.5, ex, ex - 1) + 127
    byte = np.clip(np.where(amax > 0, byte, 1), 1, 254)
    scaled = (w * np.exp2(127.0 - byte)[:, None, :]).reshape(k, n).astype(np.float32)
    by_word = np.ascontiguousarray(scaled.reshape(k // 512, 128, 4, n).transpose(0, 1, 3, 2))
    if fmt == "e4m3":
        words = by_word.astype(ml_dtypes.float8_e4m3fn).view(np.uint8)
    else:
        c = by_word.astype(ml_dtypes.float4_e2m1fn).view(np.uint8) & 0xF
        words = (c[..., 0::2] | (c[..., 1::2] << 4)).reshape(k // 512, 128, 2 * n)
    return np.ascontiguousarray(words), np.ascontiguousarray(byte.astype(np.uint8).reshape(k // 512, 16, n))


def unpack_weight(words, scales, fmt):
    g, _, n = scales.shape
    words = np.ascontiguousarray(words).reshape(g, 128, n, -1)
    if fmt == "e4m3":
        vals = words.view(ml_dtypes.float8_e4m3fn).astype(np.float64)
    else:
        nib = np.empty((g, 128, n, 4), np.uint8)
        nib[..., 0::2] = words & 0xF
        nib[..., 1::2] = words >> 4
        vals = E2M1[nib]
    vals = vals * np.repeat(np.exp2(scales.astype(np.float64) - 127.0), 8, axis=1)[..., None]
    return vals.transpose(0, 1, 3, 2).reshape(g * 512, n)


def gelu(v):
    return 0.5 * v * (1.0 + np.tanh(np.sqrt(2.0 / np.pi) * (v + 0.044715 * v**3)))


def bf(x):
    return np.asarray(x, np.float32).astype(ml_dtypes.bfloat16)


def planes(Y):
    n, m = Y.shape
    b = f64(bf(Y)).reshape(n // 32, 32, m)
    amax = np.abs(b).max(1)
    byte = np.clip(np.where(amax > 0, np.frexp(amax)[1] - 1 + 127 - 7, 1), 1, 254)
    codes = (b * np.exp2(127.0 - byte)[:, None, :]).reshape(n, m).astype(np.float32).astype(ml_dtypes.float8_e4m3fn).view(np.uint8)
    words = codes.reshape(n // 512, 128, 4, m).transpose(0, 1, 3, 2)
    return np.ascontiguousarray(words), np.ascontiguousarray(byte.astype(np.uint8).reshape(n // 512, 16, m))


K, H, N, T, S, P, Q, R = 512, 1024, 512, 4096, 2048, 1024, 512, 256

def setup_inputs():
    n = np.random.standard_normal
    s = mx_kscale(K)[:, None]
    u = mx_kscale(H)[:, None]
    tab_words, tab_scales = pack_weight(n((K, T)) * s, "e4m3")
    w1 = n((K, H)) * 1.5 / np.sqrt(K) / s
    w4 = 0.7 * n((H, N)) * np.exp(0.8 * n(N))[None, :] / np.sqrt(H) / u
    w4_words, w4_scales = pack_weight(w4, "e2m1")
    return {
        "tab_words": tab_words, "tab_scales": tab_scales,
        "offs": striped(np.random.permutation(T)[:S]),
        "pos1": striped(np.random.permutation(S)[:P]),
        "pos2": striped(np.random.permutation(S)[:P]),
        "pos3": striped(np.random.permutation(P)[:Q]),
        "pos4": striped(np.random.permutation(P)[:Q]),
        "pos5": striped(np.random.permutation(Q)[:R]),
        "pos6": striped(np.random.permutation(Q)[:R]),
        "w1": w1.astype(np.float32),
        "jury": (n((H, Q)) - 1.2).astype(np.float32),
        "gain": (u[:, 0] * np.exp(0.3 * n(H))).astype(np.float32),
        "w4_words": w4_words, "w4_scales": w4_scales,
    }

def reference(tab_words, tab_scales, offs, pos1, pos2, pos3, pos4, pos5, pos6, w1, jury, gain, w4_words, w4_scales):
    v = unpack_weight(tab_words, tab_scales, "e4m3")[:, unstriped(offs)]
    e = mxq(f64(w1), 0, "e4m3").T @ v
    h = e / (1.0 + np.exp(-e))
    a1 = h[:, unstriped(pos1)] + h[:, unstriped(pos2)]
    a2 = np.maximum(a1[:, unstriped(pos3)], a1[:, unstriped(pos4)]) + f64(jury)
    a3 = a2[:, unstriped(pos5)] * a2[:, unstriped(pos6)] * f64(gain)[:, None]
    w4 = unpack_weight(w4_words, w4_scales, "e2m1")
    y = w4.T @ mxq(a3, 0, "e4m3")
    words, scales = planes(y)
    return y, words, scales

@@ -1,0 +1,280 @@
+from contextlib import ExitStack
+
+import concourse.mybir as mybir
+
+K, H, N, T, S, P1, P2, P3 = 512, 1024, 512, 4096, 2048, 1024, 512, 256
+FLOPS = 2 * K * H * S + 2 * H * N * P3
+
+F32 = mybir.dt.float32
+BF16 = mybir.dt.bfloat16
+I32 = mybir.dt.int32
+U32 = mybir.dt.uint32
+U16 = mybir.dt.uint16
+U8 = mybir.dt.uint8
+E4M3X4 = mybir.dt.float8_e4m3fn_x4
+E2M1X4 = mybir.dt.float4_e2m1fn_x4
+ADD = mybir.AluOpType.add
+MULT = mybir.AluOpType.mult
+MAX = mybir.AluOpType.max
+SILU = mybir.ActivationFunctionType.Silu
+
+PARTS = 128
+PACK = 4
+BANK = 512
+PASSES = H // (PARTS * PACK)
+SLICES = PASSES * PACK
+HALF = P3 // 2
+
+
+def tile_list_fair_panel_bracket_kernel(
+    tc, tab_words, tab_scales, offs, pos1, pos2, pos3, pos4, pos5, pos6,
+    w1, jury, gain, w4_words, w4_scales, out_0, out_1, out_2,
+):
+    nc = tc.nc
+    with ExitStack() as ctx:
+        keep = ctx.enter_context(tc.tile_pool(name="keep", bufs=1))
+        ring = ctx.enter_context(tc.tile_pool(name="ring", bufs=2))
+        psum = ctx.enter_context(tc.psum_pool(name="psum", bufs=1))
+
+        def load_list(src, name):
+            tile = keep.tile(list(src.shape), U16, name=name)
+            nc.sync.dma_start(tile[:], src)
+            return tile
+
+        idx = load_list(offs, "idx")
+        table_scales = keep.tile([PARTS, T], U8, align_bytes=64)
+        table_scales_i32 = table_scales[:].bitcast(I32)
+        for first in (0, 16):
+            nc.sync.dma_start(table_scales_i32[first : first + 16, :], tab_scales[0].bitcast(I32))
+        nc.gpsimd.memset(table_scales_i32[32:64, :], 0)
+        nc.vector.memset(table_scales_i32[64:128, :], 0)
+
+        w1_rows = w1.rearrange("(p i) r -> p i r", i=PACK)
+
+        def load_w1(b):
+            raw = keep.tile([PARTS, PACK, BANK], F32, name="w1_raw")
+            nc.sync.dma_start(raw[:], w1_rows[:, :, b * BANK : (b + 1) * BANK])
+            return raw
+
+        w1_raw = {0: load_w1(0)}
+        table_words = keep.tile([PARTS, T], I32, tag="table_then_jury", align_bytes=64)
+        nc.sync.dma_start(table_words[:], tab_words[0].rearrange("p t i -> p (t i)").bitcast(I32))
+        p1 = load_list(pos1, "p1")
+        p2 = load_list(pos2, "p2")
+        p3 = load_list(pos3, "p3")
+        p4 = load_list(pos4, "p4")
+        p5 = load_list(pos5, "p5")
+        gain_sb = keep.tile([PARTS, PASSES, 8], F32)
+        nc.sync.dma_start(
+            gain_sb[:, :, 0:PACK], gain.rearrange("(b p t) -> p b t", b=PASSES, t=PACK)
+        )
+
+        v_scales = keep.tile([PARTS, S], U8, align_bytes=64)
+        picked_scales = keep.tile([PARTS, S], U8, align_bytes=64)
+        nc.vector.tensor_copy(picked_scales[:], table_scales[:].indirect(idx[:]))
+        for q in range(4):
+            nc.sync.dma_start(
+                v_scales[:].bitcast(I32)[32 * q : 32 * q + 4, :],
+                picked_scales[:].bitcast(I32)[4 * q : 4 * q + 4, :],
+            )
+
+        w4_raw = keep.tile([PARTS, PASSES, 2 * N], U8, align_bytes=64)
+        nc.sync.dma_start(
+            w4_raw[:].bitcast(I32), w4_words.bitcast(I32).rearrange("a p c -> p a c")
+        )
+        w4_scales_raw = keep.tile([PARTS, PASSES, N], U8, align_bytes=64)
+        nc.gpsimd.memset(w4_scales_raw[:].bitcast(I32), 0)
+        for q in range(4):
+            nc.sync.dma_start(
+                w4_scales_raw[:].bitcast(I32)[32 * q : 32 * q + 4],
+                w4_scales[:, 4 * q : 4 * q + 4, :].bitcast(I32).rearrange("a r c -> r a c"),
+            )
+        p6 = load_list(pos6, "p6")
+        chunks = S // BANK
+        v_words = [keep.tile([PARTS, BANK], U32, name=f"v_words{c}", align_bytes=64) for c in range(chunks)]
+        cols = BANK // 16
+
+        def gather_words(c):
+            nc.vector.tensor_copy(
+                v_words[c][:],
+                table_words[:].bitcast(U32).indirect(idx[:, c * cols : (c + 1) * cols]),
+            )
+
+        w1_codes = keep.tile([PARTS, H], U32, align_bytes=64)
+        w1_scales = keep.tile([PARTS, H], U8, align_bytes=64)
+
+        def quantize_w1(s):
+            b, t = divmod(s, PACK)
+            rounded = ring.tile([PARTS, PARTS, PACK], BF16, name="w1_bf16", bufs=PACK, align_bytes=64)
+            nc.scalar.copy(rounded[:], w1_raw[b][:, :, t::PACK].rearrange("p i m -> p m i"))
+            mine = slice(s * PARTS, (s + 1) * PARTS)
+            nc.vector.quantize_mx(
+                out=w1_codes[:, mine].bitcast(E4M3X4),
+                scales=w1_scales[:, mine],
+                in_=rounded[:].rearrange("p m i -> p (m i)"),
+            )
+
+        def first_product(s):
+            h = ring.tile([PARTS, S], F32, name="h", bufs=4)
+            mine = slice(s * PARTS, (s + 1) * PARTS)
+            for c in range(chunks):
+                e = psum.tile([PARTS, BANK], F32, name="e", bufs=6)
+                nc.tensor.matmul_mx(
+                    out=e[:],
+                    lhsT=w1_codes[:, mine].bitcast(E4M3X4),
+                    lhsT_scale=w1_scales[:, mine],
+                    rhs=v_words[c][:].bitcast(E4M3X4),
+                    rhs_scale=v_scales[:, c * BANK : (c + 1) * BANK],
+                    start=True,
+                    stop=True,
+                )
+                nc.scalar.activation(h[:, c * BANK : (c + 1) * BANK], e[:], SILU)
+            return h
+
+        for s in range(PACK):
+            quantize_w1(s)
+        w1_raw[1] = load_w1(1)
+        for c in range(chunks):
+            gather_words(c)
+        jury_all = keep.tile([PARTS, PASSES, PACK * P2], F32, tag="table_then_jury", align_bytes=64)
+        jury_rows = jury.rearrange("(b p t) j -> b p (t j)", b=PASSES, t=PACK)
+        for b in range(PASSES):
+            nc.sync.dma_start(jury_all[:, b, :], jury_rows[b])
+        h = {0: first_product(0)}
+
+        w4_codes = keep.tile([PARTS, PASSES, 2 * N], U8, align_bytes=64)
+        w4_planes = keep.tile([PARTS, PASSES, N], U8, align_bytes=64)
+        nc.vector.tensor_copy(
+            w4_codes[:].bitcast(U16).rearrange("p a (t m) -> p a t m", t=PACK),
+            w4_raw[:].bitcast(U16).rearrange("p a (m t) -> p a t m", t=PACK),
+        )
+        nc.vector.tensor_copy(
+            w4_planes[:].rearrange("p a (t m) -> p a t m", t=PACK),
+            w4_scales_raw[:].rearrange("p a (m t) -> p a t m", t=PACK),
+        )
+
+        gain_wide = keep.tile([PARTS, SLICES, P3], F32)
+        a3 = [[keep.tile([PARTS, PACK, HALF], F32, name=f"a3_{b}_{u}") for u in range(2)] for b in range(PASSES)]
+        y_acc = [psum.tile([PARTS, PACK, HALF], F32, name=f"y_acc{u}") for u in range(2)]
+        y_codes = keep.tile([PARTS, P3], U32, align_bytes=64)
+        y_scales = keep.tile([PARTS, P3], U8, align_bytes=64)
+        left, a1, upper, lower, a2, scaled = {}, {}, {}, {}, {}, {}
+
+        def pick_left(s):
+            left[s] = ring.tile([PARTS, P1], F32, name="left")
+            nc.vector.tensor_copy(left[s][:], h[s][:].indirect(p1[:]))
+
+        def add_right(s):
+            a1[s] = ring.tile([PARTS, P1], F32, name="a1")
+            nc.vector.tensor_tensor(a1[s][:], h[s][:].indirect(p2[:]), left[s][:], ADD)
+
+        def pick_upper(s):
+            b, t = divmod(s, PACK)
+            upper[s] = ring.tile([PARTS, P2], F32, name="upper")
+            nc.vector.tensor_tensor(upper[s][:], a1[s][:].indirect(p3[:]), jury_all[:, b, t * P2 : (t + 1) * P2], ADD)
+
+        def pick_lower(s):
+            b, t = divmod(s, PACK)
+            lower[s] = ring.tile([PARTS, P2], F32, name="lower")
+            nc.vector.tensor_tensor(lower[s][:], a1[s][:].indirect(p4[:]), jury_all[:, b, t * P2 : (t + 1) * P2], ADD)
+
+        def larger(s):
+            a2[s] = ring.tile([PARTS, P2], F32, name="a2")
+            nc.vector.tensor_tensor(a2[s][:], upper[s][:], lower[s][:], MAX)
+
+        def spread_gain(s):
+            b, t = divmod(s, PACK)
+            nc.scalar.copy(gain_wide[:, s, :], gain_sb[:, b, t : t + 1].to_broadcast([PARTS, P3]))
+
+        def pick_scaled(s):
+            scaled[s] = ring.tile([PARTS, P3], F32, name="scaled")
+            nc.vector.tensor_tensor(scaled[s][:], a2[s][:].indirect(p5[:]), gain_wide[:, s, :], MULT)
+
+        def multiply(s, u):
+            b, t = divmod(s, PACK)
+            nc.vector.tensor_tensor(
+                a3[b][u][:, t, :],
+                a2[s][:].indirect(p6[:, u * HALF // 16 : (u + 1) * HALF // 16]),
+                scaled[s][:, u * HALF : (u + 1) * HALF],
+                MULT,
+            )
+
+        def second_product(b, u):
+            rounded = ring.tile([PARTS, HALF, PACK], BF16, name="a3_bf16", align_bytes=64)
+            src = a3[b][u][:].rearrange("p t (c i) -> p c t i", i=4)
+            dst = rounded[:].rearrange("p (c i) t -> p c t i", i=4)
+            if b == PASSES - 1:
+                nc.vector.tensor_copy(dst, src)
+            else:
+                nc.scalar.copy(dst, src)
+            codes = ring.tile([PARTS, HALF], U32, name="a3_codes", align_bytes=64)
+            scales = ring.tile([PARTS, HALF], U8, name="a3_scales", align_bytes=64)
+            nc.vector.quantize_mx(
+                out=codes[:].bitcast(E4M3X4),
+                scales=scales[:],
+                in_=rounded[:].rearrange("p j t -> p (j t)"),
+            )
+            for t in range(PACK):
+                nc.tensor.matmul_mx(
+                    out=y_acc[u][:, t, :],
+                    lhsT=w4_codes[:, b, 2 * t * PARTS : 2 * (t + 1) * PARTS].bitcast(E2M1X4),
+                    lhsT_scale=w4_planes[:, b, t * PARTS : (t + 1) * PARTS],
+                    rhs=codes[:].bitcast(E4M3X4),
+                    rhs_scale=scales[:],
+                    start=(b == 0 and t == 0),
+                    stop=(b == PASSES - 1 and t == PACK - 1),
+                )
+
+        y_rows = out_0.rearrange("(p t) j -> p t j", t=PACK)
+        y_words = out_1[0].rearrange("p m t -> p (m t)").bitcast(I32)
+
+        def hand_out(u):
+            mine = slice(u * HALF, (u + 1) * HALF)
+            y = ring.tile([PARTS, PACK, HALF], F32, name="y")
+            nc.scalar.copy(y[:], y_acc[u][:])
+            nc.scalar.dma_start(y_rows[:, :, mine], y[:])
+            rounded = ring.tile([PARTS, HALF, PACK], BF16, name="y_bf16", align_bytes=64)
+            nc.vector.tensor_copy(
+                rounded[:].rearrange("p (c i) t -> p c t i", i=4),
+                y[:].rearrange("p t (c i) -> p c t i", i=4),
+            )
+            nc.vector.quantize_mx(
+                out=y_codes[:, mine].bitcast(E4M3X4),
+                scales=y_scales[:, mine],
+                in_=rounded[:].rearrange("p j t -> p (j t)"),
+            )
+            nc.sync.dma_start(y_words[:, mine], y_codes[:, mine].bitcast(I32))
+
+        for s in range(SLICES + 2):
+            if s + 1 < SLICES:
+                if s + 1 >= PACK:
+                    quantize_w1(s + 1)
+                h[s + 1] = first_product(s + 1)
+            if s < SLICES:
+                spread_gain(s)
+                pick_left(s)
+            if 2 <= s:
+                pick_scaled(s - 2)
+            if 1 <= s <= SLICES:
+                pick_upper(s - 1)
+            if 2 <= s:
+                multiply(s - 2, 0)
+                multiply(s - 2, 1)
+            if 1 <= s <= SLICES:
+                pick_lower(s - 1)
+            if s < SLICES:
+                add_right(s)
+            if 1 <= s <= SLICES:
+                larger(s - 1)
+            if s - 2 == PACK - 1:
+                second_product(0, 0)
+                second_product(0, 1)
+        for u in range(2):
+            second_product(1, u)
+            hand_out(u)
+        for q in range(4):
+            queue = nc.sync if q % 2 == 0 else nc.scalar
+            queue.dma_start(
+                out_2[0, 4 * q : 4 * q + 4, :].bitcast(I32),
+                y_scales[:].bitcast(I32)[32 * q : 32 * q + 4, :],
+            )

@@ -1,6 +1,7 @@
 from contextlib import ExitStack
 
 import concourse.mybir as mybir
+from concourse.masks import make_identity
 
 K, H, N, T, S, P1, P2, P3 = 512, 1024, 512, 4096, 2048, 1024, 512, 256
 FLOPS = 2 * K * H * S + 2 * H * N * P3
@@ -16,6 +17,8 @@ E2M1X4 = mybir.dt.float4_e2m1fn_x4
 ADD = mybir.AluOpType.add
 MULT = mybir.AluOpType.mult
 MAX = mybir.AluOpType.max
+SUBTRACT = mybir.AluOpType.subtract
+RELU = mybir.ActivationFunctionType.Relu
 SILU = mybir.ActivationFunctionType.Silu
 
 PARTS = 128
@@ -46,8 +49,14 @@ def tile_list_fair_panel_bracket_kernel(
         table_scales_i32 = table_scales[:].bitcast(I32)
         for first in (0, 16):
             nc.sync.dma_start(table_scales_i32[first : first + 16, :], tab_scales[0].bitcast(I32))
-        nc.gpsimd.memset(table_scales_i32[32:64, :], 0)
+        warm = keep.tile([PARTS, 2], F32)
+        nc.vector.memset(warm[:, 0:1], 0.0)
+        nc.scalar.activation(warm[:, 1:2], warm[:, 0:1], SILU)
+        nc.vector.memset(table_scales_i32[32:64, :], 0)
         nc.vector.memset(table_scales_i32[64:128, :], 0)
+
+        identity = keep.tile([PARTS, PARTS], F32)
+        make_identity(nc, identity[:])
 
         w1_rows = w1.rearrange("(p i) r -> p i r", i=PACK)
 
@@ -118,7 +127,7 @@ def tile_list_fair_panel_bracket_kernel(
             h = ring.tile([PARTS, S], F32, name="h", bufs=4)
             mine = slice(s * PARTS, (s + 1) * PARTS)
             for c in range(chunks):
-                e = psum.tile([PARTS, BANK], F32, name="e", bufs=6)
+                e = psum.tile([PARTS, BANK], F32, name="e", bufs=4)
                 nc.tensor.matmul_mx(
                     out=e[:],
                     lhsT=w1_codes[:, mine].bitcast(E4M3X4),
@@ -158,7 +167,12 @@ def tile_list_fair_panel_bracket_kernel(
         y_acc = [psum.tile([PARTS, PACK, HALF], F32, name=f"y_acc{u}") for u in range(2)]
         y_codes = keep.tile([PARTS, P3], U32, align_bytes=64)
         y_scales = keep.tile([PARTS, P3], U8, align_bytes=64)
-        left, a1, upper, lower, a2, scaled = {}, {}, {}, {}, {}, {}
+        left, a1, first, second, a2 = {}, {}, {}, {}, {}
+        last = SLICES - 1
+
+        def jury_of(s):
+            b, t = divmod(s, PACK)
+            return jury_all[:, b, t * P2 : (t + 1) * P2]
 
         def pick_left(s):
             left[s] = ring.tile([PARTS, P1], F32, name="left")
@@ -168,45 +182,75 @@ def tile_list_fair_panel_bracket_kernel(
             a1[s] = ring.tile([PARTS, P1], F32, name="a1")
             nc.vector.tensor_tensor(a1[s][:], h[s][:].indirect(p2[:]), left[s][:], ADD)
 
-        def pick_upper(s):
-            b, t = divmod(s, PACK)
-            upper[s] = ring.tile([PARTS, P2], F32, name="upper")
-            nc.vector.tensor_tensor(upper[s][:], a1[s][:].indirect(p3[:]), jury_all[:, b, t * P2 : (t + 1) * P2], ADD)
+        def pick_first(s):
+            if s == last:
+                first[s] = keep.tile([PARTS, P2], F32, name="first_last", tag="first_then_scaled")
+                nc.vector.tensor_tensor(first[s][:], a1[s][:].indirect(p3[:]), jury_of(s), ADD)
+            else:
+                first[s] = ring.tile([PARTS, P2], F32, name="first")
+                nc.vector.tensor_copy(first[s][:], a1[s][:].indirect(p3[:]))
 
-        def pick_lower(s):
-            b, t = divmod(s, PACK)
-            lower[s] = ring.tile([PARTS, P2], F32, name="lower")
-            nc.vector.tensor_tensor(lower[s][:], a1[s][:].indirect(p4[:]), jury_all[:, b, t * P2 : (t + 1) * P2], ADD)
+        def pick_second(s):
+            second[s] = ring.tile([PARTS, P2], F32, name="second")
+            if s == last:
+                nc.vector.tensor_tensor(second[s][:], a1[s][:].indirect(p4[:]), jury_of(s), ADD)
+            else:
+                nc.vector.tensor_tensor(second[s][:], a1[s][:].indirect(p4[:]), first[s][:], SUBTRACT)
 
         def larger(s):
-            a2[s] = ring.tile([PARTS, P2], F32, name="a2")
-            nc.vector.tensor_tensor(a2[s][:], upper[s][:], lower[s][:], MAX)
+            a2[s] = ring.tile([PARTS, P2], F32, name="a2", bufs=PACK + 1)
+            if s == last:
+                nc.vector.tensor_tensor(a2[s][:], first[s][:], second[s][:], MAX)
+                return
+            excess = ring.tile([PARTS, P2], F32, name="excess")
+            nc.scalar.activation(excess[:], second[s][:], RELU)
+            turned = psum.tile([PARTS, P2], F32, name="turned")
+            terms = (jury_of(s), first[s][:], excess[:])
+            blocks = P2 // PARTS
+            for i, term in enumerate(terms):
+                for c in range(blocks):
+                    cols128 = slice(c * PARTS, (c + 1) * PARTS)
+                    nc.tensor.matmul(
+                        turned[:, cols128], term[:, cols128], identity[:], is_transpose=True,
+                        start=(i == 0 and c == 0), stop=(i == len(terms) - 1 and c == blocks - 1),
+                    )
+            turned_sb = ring.tile([PARTS, P2], F32, name="turned_sb")
+            nc.scalar.copy(turned_sb[:], turned[:])
+            back = psum.tile([PARTS, P2], F32, name="back")
+            for c in range(blocks):
+                cols128 = slice(c * PARTS, (c + 1) * PARTS)
+                nc.tensor.transpose(back[:, cols128], turned_sb[:, cols128], identity[:])
+            nc.scalar.copy(a2[s][:], back[:])
 
         def spread_gain(s):
             b, t = divmod(s, PACK)
             nc.scalar.copy(gain_wide[:, s, :], gain_sb[:, b, t : t + 1].to_broadcast([PARTS, P3]))
 
-        def pick_scaled(s):
-            scaled[s] = ring.tile([PARTS, P3], F32, name="scaled")
-            nc.vector.tensor_tensor(scaled[s][:], a2[s][:].indirect(p5[:]), gain_wide[:, s, :], MULT)
+        def pick_scaled(s, dst, lo, hi):
+            nc.vector.tensor_tensor(
+                dst, a2[s][:].indirect(p5[:, lo // 16 : hi // 16]), gain_wide[:, s, lo:hi], MULT
+            )
 
-        def multiply(s, u):
+        def multiply(s, u, scaled_half):
             b, t = divmod(s, PACK)
             nc.vector.tensor_tensor(
                 a3[b][u][:, t, :],
                 a2[s][:].indirect(p6[:, u * HALF // 16 : (u + 1) * HALF // 16]),
-                scaled[s][:, u * HALF : (u + 1) * HALF],
+                scaled_half,
                 MULT,
             )
 
-        def second_product(b, u):
-            rounded = ring.tile([PARTS, HALF, PACK], BF16, name="a3_bf16", align_bytes=64)
-            src = a3[b][u][:].rearrange("p t (c i) -> p c t i", i=4)
-            dst = rounded[:].rearrange("p (c i) t -> p c t i", i=4)
-            if b == PASSES - 1:
+        def interleave(on_vector, dst, src):
+            dst = dst.rearrange("p (c i) t -> p c t i", i=4)
+            src = src.rearrange("p t (c i) -> p c t i", i=4)
+            if on_vector:
                 nc.vector.tensor_copy(dst, src)
             else:
                 nc.scalar.copy(dst, src)
+
+        def second_product(b, u):
+            rounded = ring.tile([PARTS, HALF, PACK], BF16, name="a3_bf16", align_bytes=64)
+            interleave(b == PASSES - 1 and u == 1, rounded[:], a3[b][u][:])
             codes = ring.tile([PARTS, HALF], U32, name="a3_codes", align_bytes=64)
             scales = ring.tile([PARTS, HALF], U8, name="a3_scales", align_bytes=64)
             nc.vector.quantize_mx(
@@ -232,12 +276,9 @@ def tile_list_fair_panel_bracket_kernel(
             mine = slice(u * HALF, (u + 1) * HALF)
             y = ring.tile([PARTS, PACK, HALF], F32, name="y")
             nc.scalar.copy(y[:], y_acc[u][:])
-            nc.scalar.dma_start(y_rows[:, :, mine], y[:])
+            nc.sync.dma_start(y_rows[:, :, mine], y[:])
             rounded = ring.tile([PARTS, HALF, PACK], BF16, name="y_bf16", align_bytes=64)
-            nc.vector.tensor_copy(
-                rounded[:].rearrange("p (c i) t -> p c t i", i=4),
-                y[:].rearrange("p t (c i) -> p c t i", i=4),
-            )
+            interleave(u == 1, rounded[:], y[:])
             nc.vector.quantize_mx(
                 out=y_codes[:, mine].bitcast(E4M3X4),
                 scales=y_scales[:, mine],
@@ -253,15 +294,17 @@ def tile_list_fair_panel_bracket_kernel(
             if s < SLICES:
                 spread_gain(s)
                 pick_left(s)
-            if 2 <= s:
-                pick_scaled(s - 2)
             if 1 <= s <= SLICES:
-                pick_upper(s - 1)
+                pick_first(s - 1)
             if 2 <= s:
-                multiply(s - 2, 0)
-                multiply(s - 2, 1)
+                width = P3 if s - 2 < PACK else HALF
+                scaled = ring.tile([PARTS, P3], F32, name="scaled")
+                pick_scaled(s - 2, scaled[:, 0:width], 0, width)
             if 1 <= s <= SLICES:
-                pick_lower(s - 1)
+                pick_second(s - 1)
+            if 2 <= s:
+                for u in range(width // HALF):
+                    multiply(s - 2, u, scaled[:, u * HALF : (u + 1) * HALF])
             if s < SLICES:
                 add_right(s)
             if 1 <= s <= SLICES:
@@ -269,9 +312,15 @@ def tile_list_fair_panel_bracket_kernel(
             if s - 2 == PACK - 1:
                 second_product(0, 0)
                 second_product(0, 1)
-        for u in range(2):
-            second_product(1, u)
-            hand_out(u)
+        second_product(1, 0)
+        hand_out(0)
+        scaled_late = keep.tile([PARTS, PACK, HALF], F32, tag="first_then_scaled")
+        for t in range(PACK):
+            pick_scaled(PACK + t, scaled_late[:, t, :], HALF, P3)
+        for t in range(PACK):
+            multiply(PACK + t, 1, scaled_late[:, t, :])
+        second_product(1, 1)
+        hand_out(1)
         for q in range(4):
             queue = nc.sync if q % 2 == 0 else nc.scalar
             queue.dma_start(

@@ -16,7 +16,6 @@ E4M3X4 = mybir.dt.float8_e4m3fn_x4
 E2M1X4 = mybir.dt.float4_e2m1fn_x4
 ADD = mybir.AluOpType.add
 MULT = mybir.AluOpType.mult
-MAX = mybir.AluOpType.max
 SUBTRACT = mybir.AluOpType.subtract
 RELU = mybir.ActivationFunctionType.Relu
 SILU = mybir.ActivationFunctionType.Silu
@@ -27,6 +26,7 @@ BANK = 512
 PASSES = H // (PARTS * PACK)
 SLICES = PASSES * PACK
 HALF = P3 // 2
+CAST_AT = 2
 
 
 def tile_list_fair_panel_bracket_kernel(
@@ -60,23 +60,21 @@ def tile_list_fair_panel_bracket_kernel(
 
         w1_rows = w1.rearrange("(p i) r -> p i r", i=PACK)
 
-        def load_w1(b):
-            raw = keep.tile([PARTS, PACK, BANK], F32, name="w1_raw")
-            nc.sync.dma_start(raw[:], w1_rows[:, :, b * BANK : (b + 1) * BANK])
-            return raw
-
-        w1_raw = {0: load_w1(0)}
+        gain_sb = keep.tile([PARTS, PASSES, 8], F32)
+        nc.sync.dma_start(
+            gain_sb[:, :, 0:PACK], gain.rearrange("(b p t) -> p b t", b=PASSES, t=PACK)
+        )
         table_words = keep.tile([PARTS, T], I32, tag="table_then_jury", align_bytes=64)
         nc.sync.dma_start(table_words[:], tab_words[0].rearrange("p t i -> p (t i)").bitcast(I32))
         p1 = load_list(pos1, "p1")
         p2 = load_list(pos2, "p2")
         p3 = load_list(pos3, "p3")
+        w1_first = keep.tile([PARTS, PACK, BANK], F32, tag="w1_then_jury")
+        nc.sync.dma_start(w1_first[:], w1_rows[:, :, 0:BANK])
+        w1_raw = {0: w1_first[:]}
         p4 = load_list(pos4, "p4")
         p5 = load_list(pos5, "p5")
-        gain_sb = keep.tile([PARTS, PASSES, 8], F32)
-        nc.sync.dma_start(
-            gain_sb[:, :, 0:PACK], gain.rearrange("(b p t) -> p b t", b=PASSES, t=PACK)
-        )
+        p6 = load_list(pos6, "p6")
 
         v_scales = keep.tile([PARTS, S], U8, align_bytes=64)
         picked_scales = keep.tile([PARTS, S], U8, align_bytes=64)
@@ -98,12 +96,12 @@ def tile_list_fair_panel_bracket_kernel(
                 w4_scales_raw[:].bitcast(I32)[32 * q : 32 * q + 4],
                 w4_scales[:, 4 * q : 4 * q + 4, :].bitcast(I32).rearrange("a r c -> r a c"),
             )
-        p6 = load_list(pos6, "p6")
         chunks = S // BANK
-        v_words = [keep.tile([PARTS, BANK], U32, name=f"v_words{c}", align_bytes=64) for c in range(chunks)]
+        v_words = {}
         cols = BANK // 16
 
         def gather_words(c):
+            v_words[c] = keep.tile([PARTS, BANK], U32, name="v_words", tag=f"v_words{c}", align_bytes=64)
             nc.vector.tensor_copy(
                 v_words[c][:],
                 table_words[:].bitcast(U32).indirect(idx[:, c * cols : (c + 1) * cols]),
@@ -112,19 +110,21 @@ def tile_list_fair_panel_bracket_kernel(
         w1_codes = keep.tile([PARTS, H], U32, align_bytes=64)
         w1_scales = keep.tile([PARTS, H], U8, align_bytes=64)
 
-        def quantize_w1(s):
-            b, t = divmod(s, PACK)
-            rounded = ring.tile([PARTS, PARTS, PACK], BF16, name="w1_bf16", bufs=PACK, align_bytes=64)
-            nc.scalar.copy(rounded[:], w1_raw[b][:, :, t::PACK].rearrange("p i m -> p m i"))
-            mine = slice(s * PARTS, (s + 1) * PARTS)
+        def quantize_w1(b, t0, t1, tag):
+            rounded = keep.tile([PARTS, t1 - t0, PARTS, PACK], BF16, name="w1_bf16", tag=tag, align_bytes=64)
+            nc.scalar.copy(
+                rounded[:].rearrange("p t m i -> p m i t"),
+                w1_raw[b].rearrange("p i (m t) -> p m i t", t=PACK)[:, :, :, t0:t1],
+            )
+            mine = slice((b * PACK + t0) * PARTS, (b * PACK + t1) * PARTS)
             nc.vector.quantize_mx(
                 out=w1_codes[:, mine].bitcast(E4M3X4),
                 scales=w1_scales[:, mine],
-                in_=rounded[:].rearrange("p m i -> p (m i)"),
+                in_=rounded[:].rearrange("p t m i -> p (t m i)"),
             )
 
         def first_product(s):
-            h = ring.tile([PARTS, S], F32, name="h", bufs=4)
+            h = ring.tile([PARTS, S], F32, name="h", bufs=SLICES)
             mine = slice(s * PARTS, (s + 1) * PARTS)
             for c in range(chunks):
                 e = psum.tile([PARTS, BANK], F32, name="e", bufs=4)
@@ -140,18 +140,34 @@ def tile_list_fair_panel_bracket_kernel(
                 nc.scalar.activation(h[:, c * BANK : (c + 1) * BANK], e[:], SILU)
             return h
 
-        for s in range(PACK):
-            quantize_w1(s)
-        w1_raw[1] = load_w1(1)
+        gains = {}
+
+        def spread_gain(s, width, tag):
+            b, t = divmod(s, PACK)
+            wide = keep.tile([PARTS, width], F32, name="gain_wide", tag=tag)
+            nc.scalar.copy(wide[:], gain_sb[:, b, t : t + 1].to_broadcast([PARTS, width]))
+            return wide
+
+        last = SLICES - 1
+        for s in range(SLICES):
+            gains[s] = spread_gain(s, P3 if s < PACK else HALF, f"gain{s}")
+        gain_last_early = spread_gain(last, HALF, "gain_then_scaled")
+
+        quantize_w1(0, 0, 1, f"v_words{chunks - 1}")
         for c in range(chunks):
             gather_words(c)
-        jury_all = keep.tile([PARTS, PASSES, PACK * P2], F32, tag="table_then_jury", align_bytes=64)
-        jury_rows = jury.rearrange("(b p t) j -> b p (t j)", b=PASSES, t=PACK)
-        for b in range(PASSES):
-            nc.sync.dma_start(jury_all[:, b, :], jury_rows[b])
         h = {0: first_product(0)}
+        quantize_w1(0, 1, PACK, "w1_then_w4")
+        jury_rows = jury.rearrange("(b p t) j -> b p t j", b=PASSES, t=PACK)
+        jury_first = keep.tile([PARTS, PACK, P2], F32, tag="w1_then_jury")
+        nc.sync.dma_start(jury_first[:], jury_rows[0])
+        second_halves = keep.tile([PARTS, 2, PACK, BANK], F32, tag="table_then_jury", align_bytes=64)
+        nc.sync.dma_start(second_halves[:, 0], w1_rows[:, :, BANK : 2 * BANK])
+        nc.sync.dma_start(second_halves[:, 1], jury_rows[1])
+        w1_raw[1] = second_halves[:, 0]
+        jury_sb = [jury_first[:], second_halves[:, 1]]
 
-        w4_codes = keep.tile([PARTS, PASSES, 2 * N], U8, align_bytes=64)
+        w4_codes = keep.tile([PARTS, PASSES, 2 * N], U8, tag="w1_then_w4", align_bytes=64)
         w4_planes = keep.tile([PARTS, PASSES, N], U8, align_bytes=64)
         nc.vector.tensor_copy(
             w4_codes[:].bitcast(U16).rearrange("p a (t m) -> p a t m", t=PACK),
@@ -162,83 +178,85 @@ def tile_list_fair_panel_bracket_kernel(
             w4_scales_raw[:].rearrange("p a (m t) -> p a t m", t=PACK),
         )
 
-        gain_wide = keep.tile([PARTS, SLICES, P3], F32)
-        a3 = [[keep.tile([PARTS, PACK, HALF], F32, name=f"a3_{b}_{u}") for u in range(2)] for b in range(PASSES)]
-        y_acc = [psum.tile([PARTS, PACK, HALF], F32, name=f"y_acc{u}") for u in range(2)]
-        y_codes = keep.tile([PARTS, P3], U32, align_bytes=64)
-        y_scales = keep.tile([PARTS, P3], U8, align_bytes=64)
-        left, a1, first, second, a2 = {}, {}, {}, {}, {}
-        last = SLICES - 1
+        for s in range(1, SLICES):
+            if s == CAST_AT:
+                quantize_w1(1, 0, PACK, "w1_second")
+            h[s] = first_product(s)
 
-        def jury_of(s):
-            b, t = divmod(s, PACK)
-            return jury_all[:, b, t * P2 : (t + 1) * P2]
+        left, a1, first, second, a2 = {}, {}, {}, {}, {}
+
+        def pieces(width, halved):
+            step = width // 2 if halved else width
+            return [(slice(lo, lo + step), slice(lo // 16, (lo + step) // 16)) for lo in range(0, width, step)]
 
         def pick_left(s):
             left[s] = ring.tile([PARTS, P1], F32, name="left")
-            nc.vector.tensor_copy(left[s][:], h[s][:].indirect(p1[:]))
+            for part, offsets in pieces(P1, s == 0):
+                nc.vector.tensor_copy(left[s][:, part], h[s][:].indirect(p1[:, offsets]))
 
         def add_right(s):
             a1[s] = ring.tile([PARTS, P1], F32, name="a1")
-            nc.vector.tensor_tensor(a1[s][:], h[s][:].indirect(p2[:]), left[s][:], ADD)
+            for part, offsets in pieces(P1, s == 0):
+                nc.vector.tensor_tensor(a1[s][:, part], h[s][:].indirect(p2[:, offsets]), left[s][:, part], ADD)
 
         def pick_first(s):
             if s == last:
                 first[s] = keep.tile([PARTS, P2], F32, name="first_last", tag="first_then_scaled")
-                nc.vector.tensor_tensor(first[s][:], a1[s][:].indirect(p3[:]), jury_of(s), ADD)
             else:
-                first[s] = ring.tile([PARTS, P2], F32, name="first")
-                nc.vector.tensor_copy(first[s][:], a1[s][:].indirect(p3[:]))
+                first[s] = ring.tile([PARTS, P2], F32, name="first", bufs=SLICES - 1)
+            for part, offsets in pieces(P2, s == last):
+                nc.vector.tensor_copy(first[s][:, part], a1[s][:].indirect(p3[:, offsets]))
 
         def pick_second(s):
-            second[s] = ring.tile([PARTS, P2], F32, name="second")
-            if s == last:
-                nc.vector.tensor_tensor(second[s][:], a1[s][:].indirect(p4[:]), jury_of(s), ADD)
+            if s == last - 1:
+                second[s] = keep.tile([PARTS, P2], F32, name="second_gate", tag="second_then_scaled")
             else:
-                nc.vector.tensor_tensor(second[s][:], a1[s][:].indirect(p4[:]), first[s][:], SUBTRACT)
+                second[s] = ring.tile([PARTS, P2], F32, name="second", bufs=SLICES - 1)
+            for part, offsets in pieces(P2, s == last):
+                nc.vector.tensor_tensor(
+                    second[s][:, part], a1[s][:].indirect(p4[:, offsets]), first[s][:, part], SUBTRACT
+                )
+
+        for s in range(SLICES + 1):
+            if s < SLICES:
+                pick_left(s)
+            if s >= 1:
+                pick_first(s - 1)
+            if s < SLICES:
+                add_right(s)
+            if s >= 1:
+                pick_second(s - 1)
+
+        blocks = [slice(c * PARTS, (c + 1) * PARTS) for c in range(P2 // PARTS)]
 
         def larger(s):
-            a2[s] = ring.tile([PARTS, P2], F32, name="a2", bufs=PACK + 1)
-            if s == last:
-                nc.vector.tensor_tensor(a2[s][:], first[s][:], second[s][:], MAX)
-                return
-            excess = ring.tile([PARTS, P2], F32, name="excess")
+            b, t = divmod(s, PACK)
+            excess = keep.tile([PARTS, P2], F32, name="excess", tag="staging", align_bytes=64)
             nc.scalar.activation(excess[:], second[s][:], RELU)
-            turned = psum.tile([PARTS, P2], F32, name="turned")
-            terms = (jury_of(s), first[s][:], excess[:])
-            blocks = P2 // PARTS
+            turned = psum.tile([PARTS, P2], F32, name="turned", bufs=1)
+            terms = (jury_sb[b][:, t, :], first[s][:], excess[:])
             for i, term in enumerate(terms):
-                for c in range(blocks):
-                    cols128 = slice(c * PARTS, (c + 1) * PARTS)
+                for c, block in enumerate(blocks):
                     nc.tensor.matmul(
-                        turned[:, cols128], term[:, cols128], identity[:], is_transpose=True,
-                        start=(i == 0 and c == 0), stop=(i == len(terms) - 1 and c == blocks - 1),
+                        turned[:, block], term[:, block], identity[:], is_transpose=True,
+                        start=(i == 0 and c == 0), stop=(i == len(terms) - 1 and c == len(blocks) - 1),
                     )
-            turned_sb = ring.tile([PARTS, P2], F32, name="turned_sb")
+            turned_sb = keep.tile([PARTS, P2], F32, name="turned_sb")
             nc.scalar.copy(turned_sb[:], turned[:])
-            back = psum.tile([PARTS, P2], F32, name="back")
-            for c in range(blocks):
-                cols128 = slice(c * PARTS, (c + 1) * PARTS)
-                nc.tensor.transpose(back[:, cols128], turned_sb[:, cols128], identity[:])
+            back = psum.tile([PARTS, P2], F32, name="back", bufs=2)
+            for block in blocks:
+                nc.tensor.transpose(back[:, block], turned_sb[:, block], identity[:])
+            a2[s] = ring.tile([PARTS, P2], F32, name="a2", tag="h", bufs=SLICES)
             nc.scalar.copy(a2[s][:], back[:])
 
-        def spread_gain(s):
-            b, t = divmod(s, PACK)
-            nc.scalar.copy(gain_wide[:, s, :], gain_sb[:, b, t : t + 1].to_broadcast([PARTS, P3]))
+        for s in range(SLICES):
+            larger(s)
 
-        def pick_scaled(s, dst, lo, hi):
-            nc.vector.tensor_tensor(
-                dst, a2[s][:].indirect(p5[:, lo // 16 : hi // 16]), gain_wide[:, s, lo:hi], MULT
-            )
+        def pick_scaled(s, dst, lo, hi, wide):
+            nc.vector.tensor_tensor(dst, a2[s][:].indirect(p5[:, lo // 16 : hi // 16]), wide, MULT)
 
-        def multiply(s, u, scaled_half):
-            b, t = divmod(s, PACK)
-            nc.vector.tensor_tensor(
-                a3[b][u][:, t, :],
-                a2[s][:].indirect(p6[:, u * HALF // 16 : (u + 1) * HALF // 16]),
-                scaled_half,
-                MULT,
-            )
+        def multiply(s, dst, lo, hi, scaled_part):
+            nc.vector.tensor_tensor(dst, a2[s][:].indirect(p6[:, lo // 16 : hi // 16]), scaled_part, MULT)
 
         def interleave(on_vector, dst, src):
             dst = dst.rearrange("p (c i) t -> p c t i", i=4)
@@ -248,37 +266,96 @@ def tile_list_fair_panel_bracket_kernel(
             else:
                 nc.scalar.copy(dst, src)
 
-        def second_product(b, u):
-            rounded = ring.tile([PARTS, HALF, PACK], BF16, name="a3_bf16", align_bytes=64)
-            interleave(b == PASSES - 1 and u == 1, rounded[:], a3[b][u][:])
-            codes = ring.tile([PARTS, HALF], U32, name="a3_codes", align_bytes=64)
-            scales = ring.tile([PARTS, HALF], U8, name="a3_scales", align_bytes=64)
+        def quantize_a3(rounded, width, name):
+            codes = keep.tile([PARTS, width], U32, name=f"codes_{name}", align_bytes=64)
+            scales = keep.tile([PARTS, width], U8, name=f"scales_{name}", align_bytes=64)
             nc.vector.quantize_mx(
                 out=codes[:].bitcast(E4M3X4),
                 scales=scales[:],
                 in_=rounded[:].rearrange("p j t -> p (j t)"),
             )
+            return codes, scales
+
+        y_early = psum.tile([PARTS, PACK, HALF], F32, tag="e", bufs=4)
+        y_late = [psum.tile([PARTS, 2, HALF], F32, name=f"y_late{k}", tag="e", bufs=4) for k in range(2)]
+
+        def second_product(b, u, codes, scales):
             for t in range(PACK):
+                if u == 0:
+                    acc, opens, closes = y_early[:, t, :], t == 0, t == PACK - 1
+                else:
+                    acc, opens, closes = y_late[t // 2][:, t % 2, :], t % 2 == 0, t % 2 == 1
                 nc.tensor.matmul_mx(
-                    out=y_acc[u][:, t, :],
+                    out=acc,
                     lhsT=w4_codes[:, b, 2 * t * PARTS : 2 * (t + 1) * PARTS].bitcast(E2M1X4),
                     lhsT_scale=w4_planes[:, b, t * PARTS : (t + 1) * PARTS],
-                    rhs=codes[:].bitcast(E4M3X4),
-                    rhs_scale=scales[:],
-                    start=(b == 0 and t == 0),
-                    stop=(b == PASSES - 1 and t == PACK - 1),
+                    rhs=codes.bitcast(E4M3X4),
+                    rhs_scale=scales,
+                    start=(b == 0 and opens),
+                    stop=(b == PASSES - 1 and closes),
                 )
+
+        a3_first = keep.tile([PARTS, PACK, P3], F32)
+        a3_early = keep.tile([PARTS, PACK, HALF], F32)
+        scaled_first = keep.tile([PARTS, PACK, P3], F32, tag="second_then_scaled")
+        scaled_early = keep.tile([PARTS, PACK + 1, HALF], F32, tag="first_then_scaled")
+
+        def scale_step(s):
+            if s < PACK:
+                pick_scaled(s, scaled_first[:, s, :], 0, P3, gains[s][:])
+            else:
+                wide = gain_last_early if s == last else gains[s]
+                pick_scaled(s, scaled_early[:, s - PACK, :], 0, HALF, wide[:])
+            if s == last:
+                pick_scaled(s, scaled_early[:, PACK, :], HALF, P3, gains[s][:])
+
+        def multiply_step(s):
+            if s < PACK:
+                multiply(s, a3_first[:, s, :], 0, P3, scaled_first[:, s, :])
+            else:
+                multiply(s, a3_early[:, s - PACK, :], 0, HALF, scaled_early[:, s - PACK, :])
+
+        scale_step(0)
+        for s in range(SLICES):
+            if s < last:
+                scale_step(s + 1)
+            multiply_step(s)
+            if s == PACK - 1:
+                rounded_first = keep.tile([PARTS, P3, PACK], BF16, tag="staging", align_bytes=64)
+                interleave(False, rounded_first[:], a3_first[:])
+                codes, scales = quantize_a3(rounded_first, P3, "first")
+                for u in range(2):
+                    mine = slice(u * HALF, (u + 1) * HALF)
+                    second_product(0, u, codes[:, mine], scales[:, mine])
+
+        rounded_early = keep.tile([PARTS, HALF, PACK], BF16, tag="rounded_then_a3", align_bytes=64)
+        interleave(False, rounded_early[:], a3_early[:])
+        codes, scales = quantize_a3(rounded_early, HALF, "early")
+        second_product(1, 0, codes[:], scales[:])
+
+        scaled_rest = keep.tile([PARTS, PACK - 1, HALF], F32, tag="gain_then_scaled")
+        for t in range(PACK - 1):
+            pick_scaled(PACK + t, scaled_rest[:, t, :], HALF, P3, gains[PACK + t][:])
+        scaled_late = [scaled_rest[:, t, :] for t in range(PACK - 1)] + [scaled_early[:, PACK, :]]
+        a3_late = [
+            keep.tile([PARTS, 2, HALF], F32, name="a3_late0"),
+            keep.tile([PARTS, 2, HALF], F32, name="a3_late1", tag="rounded_then_a3", align_bytes=64),
+        ]
+        rounded_late = keep.tile([PARTS, HALF, PACK], BF16, align_bytes=64)
+        for k in range(2):
+            for t in range(2 * k, 2 * k + 2):
+                multiply(PACK + t, a3_late[k][:, t % 2, :], HALF, P3, scaled_late[t])
+            interleave(k == 1, rounded_late[:, :, 2 * k : 2 * k + 2], a3_late[k][:])
+        codes, scales = quantize_a3(rounded_late, HALF, "late")
+        second_product(1, 1, codes[:], scales[:])
 
         y_rows = out_0.rearrange("(p t) j -> p t j", t=PACK)
         y_words = out_1[0].rearrange("p m t -> p (m t)").bitcast(I32)
+        y_codes = keep.tile([PARTS, P3], U32, align_bytes=64)
+        y_scales = keep.tile([PARTS, P3], U8, align_bytes=64)
 
-        def hand_out(u):
+        def quantize_y(u, rounded):
             mine = slice(u * HALF, (u + 1) * HALF)
-            y = ring.tile([PARTS, PACK, HALF], F32, name="y")
-            nc.scalar.copy(y[:], y_acc[u][:])
-            nc.sync.dma_start(y_rows[:, :, mine], y[:])
-            rounded = ring.tile([PARTS, HALF, PACK], BF16, name="y_bf16", align_bytes=64)
-            interleave(u == 1, rounded[:], y[:])
             nc.vector.quantize_mx(
                 out=y_codes[:, mine].bitcast(E4M3X4),
                 scales=y_scales[:, mine],
@@ -286,41 +363,21 @@ def tile_list_fair_panel_bracket_kernel(
             )
             nc.sync.dma_start(y_words[:, mine], y_codes[:, mine].bitcast(I32))
 
-        for s in range(SLICES + 2):
-            if s + 1 < SLICES:
-                if s + 1 >= PACK:
-                    quantize_w1(s + 1)
-                h[s + 1] = first_product(s + 1)
-            if s < SLICES:
-                spread_gain(s)
-                pick_left(s)
-            if 1 <= s <= SLICES:
-                pick_first(s - 1)
-            if 2 <= s:
-                width = P3 if s - 2 < PACK else HALF
-                scaled = ring.tile([PARTS, P3], F32, name="scaled")
-                pick_scaled(s - 2, scaled[:, 0:width], 0, width)
-            if 1 <= s <= SLICES:
-                pick_second(s - 1)
-            if 2 <= s:
-                for u in range(width // HALF):
-                    multiply(s - 2, u, scaled[:, u * HALF : (u + 1) * HALF])
-            if s < SLICES:
-                add_right(s)
-            if 1 <= s <= SLICES:
-                larger(s - 1)
-            if s - 2 == PACK - 1:
-                second_product(0, 0)
-                second_product(0, 1)
-        second_product(1, 0)
-        hand_out(0)
-        scaled_late = keep.tile([PARTS, PACK, HALF], F32, tag="first_then_scaled")
-        for t in range(PACK):
-            pick_scaled(PACK + t, scaled_late[:, t, :], HALF, P3)
-        for t in range(PACK):
-            multiply(PACK + t, 1, scaled_late[:, t, :])
-        second_product(1, 1)
-        hand_out(1)
+        y_rounded = keep.tile([PARTS, HALF, PACK], BF16, align_bytes=64)
+        interleave(False, y_rounded[:], y_early[:])
+        y_sb = keep.tile([PARTS, PACK, HALF], F32)
+        nc.scalar.copy(y_sb[:], y_early[:])
+        nc.sync.dma_start(y_rows[:, :, 0:HALF], y_sb[:])
+        quantize_y(0, y_rounded)
+
+        y_sb_late = keep.tile([PARTS, PACK, HALF], F32)
+        y_rounded_late = keep.tile([PARTS, HALF, PACK], BF16, align_bytes=64)
+        interleave(True, y_rounded_late[:, :, 0:2], y_late[0][:])
+        nc.scalar.copy(y_sb_late[:, 2:4, :], y_late[1][:])
+        interleave(True, y_rounded_late[:, :, 2:4], y_late[1][:])
+        nc.scalar.copy(y_sb_late[:, 0:2, :], y_late[0][:])
+        nc.scalar.dma_start(y_rows[:, :, HALF:P3], y_sb_late[:])
+        quantize_y(1, y_rounded_late)
         for q in range(4):
             queue = nc.sync if q % 2 == 0 else nc.scalar
             queue.dma_start(

from contextlib import ExitStack

import concourse.mybir as mybir
from concourse.masks import make_identity

K, H, N, T, S, P1, P2, P3 = 512, 1024, 512, 4096, 2048, 1024, 512, 256
FLOPS = 2 * K * H * S + 2 * H * N * P3

F32 = mybir.dt.float32
BF16 = mybir.dt.bfloat16
I32 = mybir.dt.int32
U32 = mybir.dt.uint32
U16 = mybir.dt.uint16
U8 = mybir.dt.uint8
E4M3X4 = mybir.dt.float8_e4m3fn_x4
E2M1X4 = mybir.dt.float4_e2m1fn_x4
ADD = mybir.AluOpType.add
MULT = mybir.AluOpType.mult
SUBTRACT = mybir.AluOpType.subtract
RELU = mybir.ActivationFunctionType.Relu
SILU = mybir.ActivationFunctionType.Silu

PARTS = 128
PACK = 4
BANK = 512
PASSES = H // (PARTS * PACK)
SLICES = PASSES * PACK
HALF = P3 // 2
CAST_AT = 2


def tile_list_fair_panel_bracket_kernel(
    tc, tab_words, tab_scales, offs, pos1, pos2, pos3, pos4, pos5, pos6,
    w1, jury, gain, w4_words, w4_scales, out_0, out_1, out_2,
):
    nc = tc.nc
    with ExitStack() as ctx:
        keep = ctx.enter_context(tc.tile_pool(name="keep", bufs=1))
        ring = ctx.enter_context(tc.tile_pool(name="ring", bufs=2))
        psum = ctx.enter_context(tc.psum_pool(name="psum", bufs=1))

        def load_list(src, name):
            tile = keep.tile(list(src.shape), U16, name=name)
            nc.sync.dma_start(tile[:], src)
            return tile

        idx = load_list(offs, "idx")
        table_scales = keep.tile([PARTS, T], U8, align_bytes=64)
        table_scales_i32 = table_scales[:].bitcast(I32)
        for first in (0, 16):
            nc.sync.dma_start(table_scales_i32[first : first + 16, :], tab_scales[0].bitcast(I32))
        warm = keep.tile([PARTS, 2], F32)
        nc.vector.memset(warm[:, 0:1], 0.0)
        nc.scalar.activation(warm[:, 1:2], warm[:, 0:1], SILU)
        nc.vector.memset(table_scales_i32[32:64, :], 0)
        nc.vector.memset(table_scales_i32[64:128, :], 0)

        identity = keep.tile([PARTS, PARTS], F32)
        make_identity(nc, identity[:])

        w1_rows = w1.rearrange("(p i) r -> p i r", i=PACK)

        gain_sb = keep.tile([PARTS, PASSES, 8], F32)
        nc.sync.dma_start(
            gain_sb[:, :, 0:PACK], gain.rearrange("(b p t) -> p b t", b=PASSES, t=PACK)
        )
        table_words = keep.tile([PARTS, T], I32, tag="table_then_jury", align_bytes=64)
        nc.sync.dma_start(table_words[:], tab_words[0].rearrange("p t i -> p (t i)").bitcast(I32))
        p1 = load_list(pos1, "p1")
        p2 = load_list(pos2, "p2")
        p3 = load_list(pos3, "p3")
        w1_first = keep.tile([PARTS, PACK, BANK], F32, tag="w1_then_jury")
        nc.sync.dma_start(w1_first[:], w1_rows[:, :, 0:BANK])
        w1_raw = {0: w1_first[:]}
        p4 = load_list(pos4, "p4")
        p5 = load_list(pos5, "p5")
        p6 = load_list(pos6, "p6")

        v_scales = keep.tile([PARTS, S], U8, align_bytes=64)
        picked_scales = keep.tile([PARTS, S], U8, align_bytes=64)
        nc.vector.tensor_copy(picked_scales[:], table_scales[:].indirect(idx[:]))
        for q in range(4):
            nc.sync.dma_start(
                v_scales[:].bitcast(I32)[32 * q : 32 * q + 4, :],
                picked_scales[:].bitcast(I32)[4 * q : 4 * q + 4, :],
            )

        w4_raw = keep.tile([PARTS, PASSES, 2 * N], U8, align_bytes=64)
        nc.sync.dma_start(
            w4_raw[:].bitcast(I32), w4_words.bitcast(I32).rearrange("a p c -> p a c")
        )
        w4_scales_raw = keep.tile([PARTS, PASSES, N], U8, align_bytes=64)
        nc.gpsimd.memset(w4_scales_raw[:].bitcast(I32), 0)
        for q in range(4):
            nc.sync.dma_start(
                w4_scales_raw[:].bitcast(I32)[32 * q : 32 * q + 4],
                w4_scales[:, 4 * q : 4 * q + 4, :].bitcast(I32).rearrange("a r c -> r a c"),
            )
        chunks = S // BANK
        v_words = {}
        cols = BANK // 16

        def gather_words(c):
            v_words[c] = keep.tile([PARTS, BANK], U32, name="v_words", tag=f"v_words{c}", align_bytes=64)
            nc.vector.tensor_copy(
                v_words[c][:],
                table_words[:].bitcast(U32).indirect(idx[:, c * cols : (c + 1) * cols]),
            )

        w1_codes = keep.tile([PARTS, H], U32, align_bytes=64)
        w1_scales = keep.tile([PARTS, H], U8, align_bytes=64)

        def quantize_w1(b, t0, t1, tag):
            rounded = keep.tile([PARTS, t1 - t0, PARTS, PACK], BF16, name="w1_bf16", tag=tag, align_bytes=64)
            nc.scalar.copy(
                rounded[:].rearrange("p t m i -> p m i t"),
                w1_raw[b].rearrange("p i (m t) -> p m i t", t=PACK)[:, :, :, t0:t1],
            )
            mine = slice((b * PACK + t0) * PARTS, (b * PACK + t1) * PARTS)
            nc.vector.quantize_mx(
                out=w1_codes[:, mine].bitcast(E4M3X4),
                scales=w1_scales[:, mine],
                in_=rounded[:].rearrange("p t m i -> p (t m i)"),
            )

        def first_product(s):
            h = ring.tile([PARTS, S], F32, name="h", bufs=SLICES)
            mine = slice(s * PARTS, (s + 1) * PARTS)
            for c in range(chunks):
                e = psum.tile([PARTS, BANK], F32, name="e", bufs=4)
                nc.tensor.matmul_mx(
                    out=e[:],
                    lhsT=w1_codes[:, mine].bitcast(E4M3X4),
                    lhsT_scale=w1_scales[:, mine],
                    rhs=v_words[c][:].bitcast(E4M3X4),
                    rhs_scale=v_scales[:, c * BANK : (c + 1) * BANK],
                    start=True,
                    stop=True,
                )
                nc.scalar.activation(h[:, c * BANK : (c + 1) * BANK], e[:], SILU)
            return h

        gains = {}

        def spread_gain(s, width, tag):
            b, t = divmod(s, PACK)
            wide = keep.tile([PARTS, width], F32, name="gain_wide", tag=tag)
            nc.scalar.copy(wide[:], gain_sb[:, b, t : t + 1].to_broadcast([PARTS, width]))
            return wide

        last = SLICES - 1
        for s in range(SLICES):
            gains[s] = spread_gain(s, P3 if s < PACK else HALF, f"gain{s}")
        gain_last_early = spread_gain(last, HALF, "gain_then_scaled")

        quantize_w1(0, 0, 1, f"v_words{chunks - 1}")
        for c in range(chunks):
            gather_words(c)
        h = {0: first_product(0)}
        quantize_w1(0, 1, PACK, "w1_then_w4")
        jury_rows = jury.rearrange("(b p t) j -> b p t j", b=PASSES, t=PACK)
        jury_first = keep.tile([PARTS, PACK, P2], F32, tag="w1_then_jury")
        nc.sync.dma_start(jury_first[:], jury_rows[0])
        second_halves = keep.tile([PARTS, 2, PACK, BANK], F32, tag="table_then_jury", align_bytes=64)
        nc.sync.dma_start(second_halves[:, 0], w1_rows[:, :, BANK : 2 * BANK])
        nc.sync.dma_start(second_halves[:, 1], jury_rows[1])
        w1_raw[1] = second_halves[:, 0]
        jury_sb = [jury_first[:], second_halves[:, 1]]

        w4_codes = keep.tile([PARTS, PASSES, 2 * N], U8, tag="w1_then_w4", align_bytes=64)
        w4_planes = keep.tile([PARTS, PASSES, N], U8, align_bytes=64)
        nc.vector.tensor_copy(
            w4_codes[:].bitcast(U16).rearrange("p a (t m) -> p a t m", t=PACK),
            w4_raw[:].bitcast(U16).rearrange("p a (m t) -> p a t m", t=PACK),
        )
        nc.vector.tensor_copy(
            w4_planes[:].rearrange("p a (t m) -> p a t m", t=PACK),
            w4_scales_raw[:].rearrange("p a (m t) -> p a t m", t=PACK),
        )

        for s in range(1, SLICES):
            if s == CAST_AT:
                quantize_w1(1, 0, PACK, "w1_second")
            h[s] = first_product(s)

        left, a1, first, second, a2 = {}, {}, {}, {}, {}

        def pieces(width, halved):
            step = width // 2 if halved else width
            return [(slice(lo, lo + step), slice(lo // 16, (lo + step) // 16)) for lo in range(0, width, step)]

        def pick_left(s):
            left[s] = ring.tile([PARTS, P1], F32, name="left")
            for part, offsets in pieces(P1, s == 0):
                nc.vector.tensor_copy(left[s][:, part], h[s][:].indirect(p1[:, offsets]))

        def add_right(s):
            a1[s] = ring.tile([PARTS, P1], F32, name="a1")
            for part, offsets in pieces(P1, s == 0):
                nc.vector.tensor_tensor(a1[s][:, part], h[s][:].indirect(p2[:, offsets]), left[s][:, part], ADD)

        def pick_first(s):
            if s == last:
                first[s] = keep.tile([PARTS, P2], F32, name="first_last", tag="first_then_scaled")
            else:
                first[s] = ring.tile([PARTS, P2], F32, name="first", bufs=SLICES - 1)
            for part, offsets in pieces(P2, s == last):
                nc.vector.tensor_copy(first[s][:, part], a1[s][:].indirect(p3[:, offsets]))

        def pick_second(s):
            if s == last - 1:
                second[s] = keep.tile([PARTS, P2], F32, name="second_gate", tag="second_then_scaled")
            else:
                second[s] = ring.tile([PARTS, P2], F32, name="second", bufs=SLICES - 1)
            for part, offsets in pieces(P2, s == last):
                nc.vector.tensor_tensor(
                    second[s][:, part], a1[s][:].indirect(p4[:, offsets]), first[s][:, part], SUBTRACT
                )

        for s in range(SLICES + 1):
            if s < SLICES:
                pick_left(s)
            if s >= 1:
                pick_first(s - 1)
            if s < SLICES:
                add_right(s)
            if s >= 1:
                pick_second(s - 1)

        blocks = [slice(c * PARTS, (c + 1) * PARTS) for c in range(P2 // PARTS)]

        def larger(s):
            b, t = divmod(s, PACK)
            excess = keep.tile([PARTS, P2], F32, name="excess", tag="staging", align_bytes=64)
            nc.scalar.activation(excess[:], second[s][:], RELU)
            turned = psum.tile([PARTS, P2], F32, name="turned", bufs=1)
            terms = (jury_sb[b][:, t, :], first[s][:], excess[:])
            for i, term in enumerate(terms):
                for c, block in enumerate(blocks):
                    nc.tensor.matmul(
                        turned[:, block], term[:, block], identity[:], is_transpose=True,
                        start=(i == 0 and c == 0), stop=(i == len(terms) - 1 and c == len(blocks) - 1),
                    )
            turned_sb = keep.tile([PARTS, P2], F32, name="turned_sb")
            nc.scalar.copy(turned_sb[:], turned[:])
            back = psum.tile([PARTS, P2], F32, name="back", bufs=2)
            for block in blocks:
                nc.tensor.transpose(back[:, block], turned_sb[:, block], identity[:])
            a2[s] = ring.tile([PARTS, P2], F32, name="a2", tag="h", bufs=SLICES)
            nc.scalar.copy(a2[s][:], back[:])

        for s in range(SLICES):
            larger(s)

        def pick_scaled(s, dst, lo, hi, wide):
            nc.vector.tensor_tensor(dst, a2[s][:].indirect(p5[:, lo // 16 : hi // 16]), wide, MULT)

        def multiply(s, dst, lo, hi, scaled_part):
            nc.vector.tensor_tensor(dst, a2[s][:].indirect(p6[:, lo // 16 : hi // 16]), scaled_part, MULT)

        def interleave(on_vector, dst, src):
            dst = dst.rearrange("p (c i) t -> p c t i", i=4)
            src = src.rearrange("p t (c i) -> p c t i", i=4)
            if on_vector:
                nc.vector.tensor_copy(dst, src)
            else:
                nc.scalar.copy(dst, src)

        def quantize_a3(rounded, width, name):
            codes = keep.tile([PARTS, width], U32, name=f"codes_{name}", align_bytes=64)
            scales = keep.tile([PARTS, width], U8, name=f"scales_{name}", align_bytes=64)
            nc.vector.quantize_mx(
                out=codes[:].bitcast(E4M3X4),
                scales=scales[:],
                in_=rounded[:].rearrange("p j t -> p (j t)"),
            )
            return codes, scales

        y_early = psum.tile([PARTS, PACK, HALF], F32, tag="e", bufs=4)
        y_late = [psum.tile([PARTS, 2, HALF], F32, name=f"y_late{k}", tag="e", bufs=4) for k in range(2)]

        def second_product(b, u, codes, scales):
            for t in range(PACK):
                if u == 0:
                    acc, opens, closes = y_early[:, t, :], t == 0, t == PACK - 1
                else:
                    acc, opens, closes = y_late[t // 2][:, t % 2, :], t % 2 == 0, t % 2 == 1
                nc.tensor.matmul_mx(
                    out=acc,
                    lhsT=w4_codes[:, b, 2 * t * PARTS : 2 * (t + 1) * PARTS].bitcast(E2M1X4),
                    lhsT_scale=w4_planes[:, b, t * PARTS : (t + 1) * PARTS],
                    rhs=codes.bitcast(E4M3X4),
                    rhs_scale=scales,
                    start=(b == 0 and opens),
                    stop=(b == PASSES - 1 and closes),
                )

        a3_first = keep.tile([PARTS, PACK, P3], F32)
        a3_early = keep.tile([PARTS, PACK, HALF], F32)
        scaled_first = keep.tile([PARTS, PACK, P3], F32, tag="second_then_scaled")
        scaled_early = keep.tile([PARTS, PACK + 1, HALF], F32, tag="first_then_scaled")

        def scale_step(s):
            if s < PACK:
                pick_scaled(s, scaled_first[:, s, :], 0, P3, gains[s][:])
            else:
                wide = gain_last_early if s == last else gains[s]
                pick_scaled(s, scaled_early[:, s - PACK, :], 0, HALF, wide[:])
            if s == last:
                pick_scaled(s, scaled_early[:, PACK, :], HALF, P3, gains[s][:])

        def multiply_step(s):
            if s < PACK:
                multiply(s, a3_first[:, s, :], 0, P3, scaled_first[:, s, :])
            else:
                multiply(s, a3_early[:, s - PACK, :], 0, HALF, scaled_early[:, s - PACK, :])

        scale_step(0)
        for s in range(SLICES):
            if s < last:
                scale_step(s + 1)
            multiply_step(s)
            if s == PACK - 1:
                rounded_first = keep.tile([PARTS, P3, PACK], BF16, tag="staging", align_bytes=64)
                interleave(False, rounded_first[:], a3_first[:])
                codes, scales = quantize_a3(rounded_first, P3, "first")
                for u in range(2):
                    mine = slice(u * HALF, (u + 1) * HALF)
                    second_product(0, u, codes[:, mine], scales[:, mine])

        rounded_early = keep.tile([PARTS, HALF, PACK], BF16, tag="rounded_then_a3", align_bytes=64)
        interleave(False, rounded_early[:], a3_early[:])
        codes, scales = quantize_a3(rounded_early, HALF, "early")
        second_product(1, 0, codes[:], scales[:])

        scaled_rest = keep.tile([PARTS, PACK - 1, HALF], F32, tag="gain_then_scaled")
        for t in range(PACK - 1):
            pick_scaled(PACK + t, scaled_rest[:, t, :], HALF, P3, gains[PACK + t][:])
        scaled_late = [scaled_rest[:, t, :] for t in range(PACK - 1)] + [scaled_early[:, PACK, :]]
        a3_late = [
            keep.tile([PARTS, 2, HALF], F32, name="a3_late0"),
            keep.tile([PARTS, 2, HALF], F32, name="a3_late1", tag="rounded_then_a3", align_bytes=64),
        ]
        rounded_late = keep.tile([PARTS, HALF, PACK], BF16, align_bytes=64)
        for k in range(2):
            for t in range(2 * k, 2 * k + 2):
                multiply(PACK + t, a3_late[k][:, t % 2, :], HALF, P3, scaled_late[t])
            interleave(k == 1, rounded_late[:, :, 2 * k : 2 * k + 2], a3_late[k][:])
        codes, scales = quantize_a3(rounded_late, HALF, "late")
        second_product(1, 1, codes[:], scales[:])

        y_rows = out_0.rearrange("(p t) j -> p t j", t=PACK)
        y_words = out_1[0].rearrange("p m t -> p (m t)").bitcast(I32)
        y_codes = keep.tile([PARTS, P3], U32, align_bytes=64)
        y_scales = keep.tile([PARTS, P3], U8, align_bytes=64)

        def quantize_y(u, rounded):
            mine = slice(u * HALF, (u + 1) * HALF)
            nc.vector.quantize_mx(
                out=y_codes[:, mine].bitcast(E4M3X4),
                scales=y_scales[:, mine],
                in_=rounded[:].rearrange("p j t -> p (j t)"),
            )
            nc.sync.dma_start(y_words[:, mine], y_codes[:, mine].bitcast(I32))

        y_rounded = keep.tile([PARTS, HALF, PACK], BF16, align_bytes=64)
        interleave(False, y_rounded[:], y_early[:])
        y_sb = keep.tile([PARTS, PACK, HALF], F32)
        nc.scalar.copy(y_sb[:], y_early[:])
        nc.sync.dma_start(y_rows[:, :, 0:HALF], y_sb[:])
        quantize_y(0, y_rounded)

        y_sb_late = keep.tile([PARTS, PACK, HALF], F32)
        y_rounded_late = keep.tile([PARTS, HALF, PACK], BF16, align_bytes=64)
        interleave(True, y_rounded_late[:, :, 0:2], y_late[0][:])
        nc.scalar.copy(y_sb_late[:, 2:4, :], y_late[1][:])
        interleave(True, y_rounded_late[:, :, 2:4], y_late[1][:])
        nc.scalar.copy(y_sb_late[:, 0:2, :], y_late[0][:])
        nc.scalar.dma_start(y_rows[:, :, HALF:P3], y_sb_late[:])
        quantize_y(1, y_rounded_late)
        for q in range(4):
            queue = nc.sync if q % 2 == 0 else nc.scalar
            queue.dma_start(
                out_2[0, 4 * q : 4 * q + 4, :].bitcast(I32),
                y_scales[:].bitcast(I32)[32 * q : 32 * q + 4, :],
            )
